import numpy as np, ml_dtypes
CORES = [13,21,141,149]
N = 4
BF = ml_dtypes.bfloat16
def gentries(a):
    return np.ascontiguousarray(a.reshape(8, 16, -1).transpose(0, 2, 1)).reshape(8, -1)
def gtable(e):
    e = np.asarray(e); return np.ascontiguousarray(e.reshape(8, -1, 16).transpose(0, 2, 1)).reshape(128, -1).astype(np.int32)
W, U, RO, D, EPS, NR = 1536, 256, 3, 200, 80, 2
S0 = W - 1 - RO * D
TOP = 784
def parts(rng):
    h = (rng.random((N, 8, 16, W)) * (1 + rng.integers(4, 8, (N, 8, 1, W)))).astype(np.int64)
    v = (0.75 + 0.5 * rng.random((N, 128, W))) * np.where(rng.random((N, 128, W)) < 0.125, -1.0, 1.0)
    f = rng.integers(1, D + 1, (N, 8, 16, W)); f[:, ::2] = np.sort(f[:, ::2], axis=2)
    w = ((D + 1) * rng.random((N, 8, 16, W)) ** 1.5).astype(np.int64)
    c = np.clip(rng.integers(0, S0 + 1, (N, 1, U)) + rng.integers(0, 97, (N, 8, U)), 0, S0)
    c = np.where(rng.random((N, 8, U)) < 0.02, rng.integers(0, S0 + 1, (N, 8, U)), c)
    tk = rng.integers(0, W, (N, 8, RO, U))
    lim = rng.integers(60, 300, (N, 1, U)) + rng.integers(-40, 41, (N, 8, U))
    return h, v, f, w, c, tk, lim
def pack(h, v, f, w, c, tk, lim):
    w = np.array(w); w[:, :, 0] = 0
    big = lambda a: np.ascontiguousarray(a.reshape(N, 128, W)).astype(np.float32).astype(BF)
    return {"hk": big(h), "vv": np.asarray(v, np.float32).astype(BF), "fw": big(f), "bw": big(w), "cur": np.stack([gtable(a) for a in c]),
            "tok": np.stack([gtable(a.reshape(8, -1)) for a in tk]), "th": np.ascontiguousarray(lim).astype(np.int32)}
def setup_inputs(rng):
    return pack(*parts(rng))
def setup_inputs_spread(rng):
    h, v, f, w, c, tk, lim = parts(rng)
    h = (rng.random((N, 8, 16, W)) * (1 + rng.integers(0, 8, (N, 8, 1, W)))).astype(np.int64)
    size = np.where(rng.random((N, 1, W)) < 0.1875, 0.5, 1.0)
    v = (0.75 + 0.25 * rng.random((N, 128, W))) * np.where(rng.random((N, 128, W)) < 0.03125, -1.0, 1.0) * size
    f = np.minimum(1 + (D * rng.random(f.shape) ** np.exp2(rng.integers(-1, 3, (N, 8, 1, W)))).astype(np.int64), D)
    w = np.minimum(((D + 1) * rng.random(w.shape) ** np.exp2(rng.integers(-1, 3, (N, 8, 1, W)))).astype(np.int64), D)
    c = np.where(rng.random((N, 1, U)) < 0.3, rng.integers(0, S0 + 1, (N, 8, U)), c)
    lim = np.minimum(np.exp2(9.62 * rng.random((N, 8, U))).astype(np.int64), TOP)
    return pack(h, v, f, w, c, tk, lim)
def setup_inputs_ends(rng):
    h, v, f, w, c, tk, lim = parts(rng)
    kind = rng.integers(0, 4, (N, 8, 1, W)); e = 7 * rng.integers(0, 2, (N, 8, 16, W))
    h = np.where(kind == 0, 7, np.where(kind == 1, 0, np.where(kind == 2, e, h)))
    f = np.where(rng.random(f.shape) < 0.8, np.where(rng.random(f.shape) < 0.5, 1, D), f)
    w = np.where(rng.random(w.shape) < 0.8, D * rng.integers(0, 2, w.shape), w)
    k = rng.random((N, 1, U))
    c = np.where(k < 0.5, S0 * rng.integers(0, 2, (N, 1, U)), np.where(k < 0.8, S0 * rng.integers(0, 2, (N, 8, U)), c))
    tk = np.where(rng.random(tk.shape) < 0.8, (W - 1) * rng.integers(0, 2, tk.shape), tk)
    lim = rng.choice(np.array([0, TOP, 0, TOP, 0, TOP, 0, TOP, TOP - 1, 392, 343, 49]), (N, 8, U))
    pos = S0 + D * np.arange(RO + 1)
    h[:, ::2, :, 0] = 0; h[:, 1::2, :, 0] = 7 * rng.integers(0, 2, (N, 4, 16)); h[:, :, :, pos[1:]] = 7
    f[:, :, 15, pos[:RO]] = D; w[:, :, 1:, W - 1] = 0; w[:, :, 1:, S0 + D] = D
    for u in (0, 3, U - 1): c[:, :, u] = S0; tk[:, :, :, u] = W - 1; lim[:, :, u] = TOP
    for u in (1, U - 2): c[:, :, u] = 0; tk[:, :, :, u] = 0; lim[:, :, u] = 0
    return pack(h, v, f, w, c, tk, lim)
def setup_inputs_corners(rng):
    h, v, f, w, c, tk, lim = parts(rng)
    h[:, 0::4] = rng.integers(1, 8, (N, 2, 1, W)); h[:, 1::4] = rng.integers(0, 2, (N, 2, 16, W)); h[:, 3::4] = rng.integers(6, 8, (N, 2, 16, W))
    lim[:, 0::4] = 16 * rng.integers(0, 8, (N, 2, U)) * rng.integers(0, 8, (N, 2, U)); lim[:, 1::4] = rng.integers(0, 12, (N, 2, U)); lim[:, 3::4] = rng.integers(600, TOP + 1, (N, 2, U))
    x = np.array([D, D - EPS, D - EPS - 1, D - EPS, D - EPS - 1, D - EPS + 1, 1, D])
    f[:, :, 15] = np.stack([rng.permutation(x) for _ in range(N)])[:, :, None]
    f[:, :, 0] = rng.choice(np.array([1, 2, 3, D - 1, D]), (N, 8, W))
    kind = rng.integers(0, 6, (N, 8, 1, W))
    w[:, :, 1:] = np.where(kind == 0, 0, np.where(kind == 1, D, rng.choice(np.array([0, 1, 2, 3, D - EPS - 1, D - EPS, D - 1, D]), (N, 8, 15, W))))
    c[:, :, 0::3] = c[:, :1, 0::3] + 0; lim[:, :, 0::3] = TOP
    c[:, :, 1::3] = S0 * rng.integers(0, 2, c[:, :, 1::3].shape)
    lim[:, :, 2::6] = 0
    return pack(h, v, f, w, c, tk, lim)
def setup_inputs_calm(rng):
    h, v, f, w, c, tk, lim = parts(rng)
    h[:, ::2] = rng.integers(0, 2, (N, 4, 16, W)); lim[:, ::2] = rng.integers(0, 9, (N, 4, U))
    near = np.arange(W) < S0
    f = np.where(near, rng.integers(1, 4, f.shape), rng.integers(D - 1, D + 1, f.shape))
    w = np.where(near, rng.integers(0, 4, w.shape), rng.choice(np.array([0, D - 2, D - 1, D]), w.shape))
    low = rng.random((N, 1, U)) < 0.7; low[:, :, 0] = True; low[:, :, U - 2] = False
    c = np.where(low, rng.integers(0, 4, (N, 1, U)) + rng.integers(0, 4, (N, 8, U)), S0)
    c[:, 7, 15::16] = S0
    tk[:, 2] = rng.integers(0, W, (N, RO, 1)); tk[:, 5] = rng.integers(0, W, (N, RO, 1))
    return pack(h, v, f, w, c, tk, lim)
def check_ranges(d):
    bad = []
    for k, lo, hi in (("hk", 0, 7), ("fw", 1, D), ("bw", 0, D), ("cur", 0, S0), ("tok", 0, W - 1), ("th", 0, TOP)):
        a = np.asarray(d[k]).astype(np.float64)
        if not (np.min(a) >= lo and np.max(a) <= hi): bad.append("range of " + k)
        if np.any(a != np.floor(a)): bad.append("whole numbers in " + k)
    if np.any(np.asarray(d["bw"]).astype(np.float64)[:, ::16] != 0): bad.append("entry 0 of bw is 0")
    a = np.abs(np.asarray(d["vv"]).astype(np.float64))
    if not np.all((a >= 0.25) & (a <= 2.0)): bad.append("sizes in vv")
    return bad
def score(h, fr, q):
    return np.matmul(h[np.arange(8)[:, None, None], fr], q[:, :, :, None])[:, :, :, 0]
def reference(hk, vv, fw, bw, cur, tok, th):
    turn = lambda a: np.ascontiguousarray(a.astype(np.float64).reshape(N, 8, 16, W).transpose(0, 1, 3, 2))
    h, v = turn(hk), turn(vv); f, w = turn(fw).astype(np.int64), turn(bw).astype(np.int64)
    c0 = np.stack([gentries(a) for a in cur]).astype(np.int64)
    tk = np.stack([gentries(a) for a in tok]).astype(np.int64).reshape(N, 8, RO, U)
    g1 = np.arange(8)[:, None]; g2 = np.arange(8)[:, None, None]
    carry = np.zeros((N, 8, U, 16))
    ym = np.zeros((N, 8, RO, U)); ys = np.zeros((N, 8, RO, U)); ya = np.zeros((N, 8, 16, RO, U))
    for t in range(RO):
        for r in range(N):
            p = (r + t) % N; c = c0[r]
            q = np.maximum(carry[r], h[p][g1, tk[r, :, t]])
            fr = c[:, :, None] + f[p][g1, c]
            hit = score(h[p], fr, q) > th[p][:, :, None]
            i = np.where(np.any(hit, axis=2), np.argmax(hit, axis=2), 15)
            stop = np.take_along_axis(fr, i[:, :, None], 2)[:, :, 0]
            last = np.max(stop, axis=0)
            b = np.where(stop < last - EPS, last, stop)
            s, back = [], []
            for k in range(NR):
                x = (p + k) % N; d = w[x][g1, b]
                at = np.maximum(b[:, :, None] - d, 0); back.append(at)
                s.append(np.where(d < (b - c)[:, :, None], score(h[x], at, q), -1.0))
            al = np.concatenate(s, axis=2); m = np.max(al, axis=2)
            e = np.where(al >= 0, np.exp((al - m[:, :, None]) * 0.0078125), 0.0)
            ym[p, :, t] = m; ys[p, :, t] = np.sum(e, axis=2)
            for k in range(NR):
                x = (p + k) % N
                part = np.matmul(e[:, :, None, 16 * k:16 * k + 16], v[x][g2, back[k]])[:, :, 0]
                ya[p][:, :, t] += part.transpose(0, 2, 1)
            if t + 1 < RO:
                j = np.argmax(s[0], axis=2)
                carry[r] = h[p][g1, np.take_along_axis(back[0], j[:, :, None], 2)[:, :, 0]]
                c0[r] = b
    return {"ym": ym.reshape(N, 8, RO * U).astype(np.float32), "ys": ys.reshape(N, 8, RO * U).astype(np.float32), "ya": ya.reshape(N, 128, RO * U).astype(np.float32)}

def check_inputs(d):
    bad = list(check_ranges(d))
    if not bad:
        for name, y in reference(**d).items():
            for q in range(N):
                v = np.abs(np.asarray(y[q], np.float64)); s = np.sqrt(np.mean(v * v))
                if v.max() > 4 * s or s < 2.0 ** 2: bad.append('%s of rank %d is uneven or too small' % (name, q))
    return bad

import numpy as np
from concourse.bass import DstId, RemoteDMATransfer
from concourse.mybir import AluOpType as ALU
from concourse.mybir import ActivationFunctionType as ACT

W, U, RO, PAD = 1536, 256, 3, 16
CH = 1024
OPT = {"parts": [[(0,), (1,)], [(0, 1)], [(0, 1)]],
       "qpool": [], "seed": 419, "slack": 200.0, "noise": 3000.0, "vdve": [], "early": [], "tries": 36000, "heat": 300.0,
       "moves": [33, 39, 43, 47, 57, 160, 240, 246, 288, 337, 463, 529, 615, 721, 735, 737, 745, 869, 1100, 1231]}
SPREAD = [{}, {"g": 1.1, "cross": 200.0, "same": 120.0, "msg": 1.4, "tab": 1.4, "ld": 1.2},
          {"g": 2.0, "pe": 0.5, "msg": 0.8, "tab": 0.8}, {"pe": 0.8, "cross": 300.0, "same": 180.0, "msg": 1.5, "tab": 1.5, "ld": 1.2}]
MODEL = {"cyc": 1.04, "g": 1.5, "pe": 0.55, "dve": 60.0, "act": 90.0, "same": 60.0, "cross": 110.0, "msg": 1.0, "tab": 1.0, "ld": 1.0}
F32, BF, I32, U16 = "float32", "bfloat16", "int32", "uint16"
POOLS = {"ps": 4, "pd": 2, "prod": 4, "qrep": 2, "vg": 8, "st": 3, "rt": 4}

SCRATCH = {}
for _n in ("K0", "K1", "V0", "V1"):
    SCRATCH[_n] = ("sbuf", [128, W + PAD], BF)
for _n in ("FW", "B0", "B1"):
    SCRATCH[_n] = ("sbuf", [128, W], BF)
for _n, _c, _d in (
        ("curi", 16, I32), ("toki", 48, I32), ("tokn", 16, I32), ("toku", 48, U16), ("thi", 256, I32), ("thT", 256, F32),
        ("ni", 256, I32), ("LIST", 256, U16), ("NL", 256, F32), ("NG", 128, F32), ("NF", 144, F32), ("pi32", 8, I32),
        ("col", 8, F32), ("MASK", 256, F32), ("RST", 256, F32), ("BD", 128, BF), ("NBD", 128, BF), ("G1", 8, BF),
        ("G4", 8, BF), ("Gf", 8, F32), ("NGf", 8, F32), ("If", 128, F32), ("Ib", 128, BF), ("I2", 128, BF), ("I8", 128, BF),
        ("J", 128, BF), ("NJ", 128, BF), ("J2", 128, BF), ("DM", 128, BF), ("F", 144, BF), ("GT", 128, BF),
        ("NGT", 128, BF), ("NGTf", 128, F32), ("THS", 128, F32), ("LAST", 128, BF), ("SEL", 128, F32), ("PRIO", 128, BF),
        ("BDf", 128, F32), ("NBDf", 128, F32), ("LASTf", 128, F32), ("thU", 256, F32),
        ("ONEb", 128, BF), ("ONEf", 256, F32), ("NEG", 128, BF), ("RS9", 16, F32), ("ZB", 128, BF), ("ZF", 128, F32),
        ("X0", 256, F32), ("cL", 48, U16), ("bL", 48, U16), ("fL", 32, U16), ("LA", 32, F32), ("MA", 32, F32),
        ("LH", 64, BF), ("HL", 96, BF), ("bU", 48, F32),
        ("q", 768, BF), ("qn", 512, BF), ("kt", 512, BF), ("f", 768, BF), ("oS", 768, U16), ("o0", 768, U16),
        ("o1", 768, U16), ("nh", 768, BF), ("sc", 864, F32), ("Bs", 96, F32), ("tm", 48, F32), ("d0", 768, BF),
        ("d1", 768, BF), ("s0", 768, BF), ("s1", 768, BF), ("X2", 768, F32), ("X3", 512, F32), ("k0", 768, F32),
        ("k1", 768, F32), ("ki", 32, I32), ("ds", 32, I32), ("mk", 48, F32), ("mi", 48, I32), ("mf", 48, F32),
        ("w0", 768, F32), ("w1", 768, F32), ("x0", 768, F32), ("cT", 768, BF), ("bT", 768, BF),
        ("mT", 768, F32), ("sT", 768, F32)):
    SCRATCH[_n] = ("sbuf", [128, _c], _d)
for _n, _w, _c, _d in (("pd", "psum", CH, F32), ("ps", "psum", 512, F32), ("prod", "sbuf", PAD + 4096, BF),
                       ("qrep", "sbuf", 4096, BF), ("vg", "sbuf", CH, BF), ("st", "sbuf", 4096, F32), ("rt", "sbuf", CH, F32)):
    for _i in range(POOLS[_n]):
        SCRATCH["%s%d" % (_n, _i)] = (_w, [128, _c], _d)

SEMAPHORES = ["pe", "dve", "act", "pool", "sent", "tK", "tB", "tV", "mtok"]
SEMAPHORES += ["ld%d" % _i for _i in range(8)]
for _t in range(RO):
    for _p in range(2):
        SEMAPHORES += ["mA%d%d" % (_t, _p), "mB%d%d" % (_t, _p), "oa%d%d" % (_t, _p), "om%d%d" % (_t, _p), "os%d%d" % (_t, _p)]

CTX = {}
PLAN = []


def split(engines, k):
    n = 1
    while 2 * n * k <= len(engines):
        n *= 2
    return [sum(1 << e for e in engines[n * j:n * j + n]) for j in range(k)]


def bits(m):
    return bin(m).count("1")


def remote(q, T, topo, src, jobs, sem):
    masks = split(topo.engines(src, jobs[0][0]), len(jobs))
    if len(jobs) == 1:
        rid, pid = topo.addr(jobs[0][0], src)
        q.remote_dma(jobs[0][1], jobs[0][2], T.sem[sem], T.sem.sent, pid, rid, masks[0])
    else:
        tr = []
        for (c, out, in_), m in zip(jobs, masks):
            rid, pid = topo.addr(c, src)
            tr.append(RemoteDMATransfer(dst_ids=[DstId(rid=rid, pnc=pid)], dma_engine_mask=m, remote_sem=T.sem[sem], src=in_, dst=out))
        q.remote_dma_fused(tr, local_sem=T.sem.sent)
    return sum(bits(m) for m in masks)


def build():
    ops, writer = [], {}
    B = lambda name: CTX["T"][name]
    P = lambda tile: CTX["T"]["%s%d" % (tile["pool"], tile["phys"])]

    def tile(pool):
        return {"pool": pool, "phys": None, "ops": [], "prev": []}

    def op(eng, fn, cost, r=(), w=(), tiles=(), lat=(0.0, "ld"), sem=None, inc=1, after=(), msg=None):
        o = {"n": len(ops), "eng": eng, "fn": fn, "cf": cost, "lf": lat, "sem": sem, "inc": inc, "tiles": list(tiles),
             "deps": set(writer[k] for k in r), "time": set(after), "msg": msg, "soft": set()}
        for tl in tiles:
            if tl["pool"] in ("ps", "pd") and tl["ops"]:
                d = tl["ops"][-1]
                if ops[d]["eng"] == eng and d not in o["deps"]:
                    o["soft"].add(d)
                o["deps"].add(d)
            tl["ops"].append(o["n"])
        for k in w:
            writer[k] = o["n"]
        ops.append(o)
        return o["n"]

    def dve(fn, n, r, w, tiles=(), c=1.0):
        return op("dve", fn, (n, c), r, w, tiles)

    def act(fn, n, r, w, tiles=(), c=1.0):
        return op("act", fn, (n, c), r, w, tiles)

    def pe(mk, cyc, r, tiles, w=(), after=()):
        def fn(q):
            last = None
            for a in mk():
                last = q.matmul(a[0], a[1], a[2], a[3], a[4])
            return last
        return op("pe", fn, (cyc, 1.0), r, w, tiles, after=after)

    def dma(eng, out, in_, sem, r, w, lat):
        return op(eng, lambda q: q.dma_start(out(), in_()), 60, r, w, lat=(lat, "ld"), sem=sem, inc=16)

    GA = "g"
    V = lambda name, a, b, s=1: (lambda: B(name)[:, a:b:s] if s > 1 else B(name)[:, a:b])
    V8 = lambda name, a, b, p=8: (lambda: B(name)[0:p, a:b])
    C = lambda j: (lambda: B("col")[:, j:j + 1])
    C8 = lambda j, p=8: (lambda: B("col")[0:p, j:j + 1])
    dma("sync", V("K0", PAD, PAD + W), lambda: B("hk")[:], "ld2", (), ["K0"], 3500)
    dma("act", V("FW", 0, W), lambda: B("fw")[:], "ld3", (), ["FW"], 3500)
    dma("sync", V("curi", 0, 16), lambda: B("cur")[:], "ld0", (), ["curi"], 2500)
    dma("act", V("toki", 0, 48), lambda: B("tok")[:], "ld1", (), ["toki"], 2500)
    dma("sync", V8("thi", 0, 256), lambda: B("th")[:], "ld4", (), ["thi"], 4000)
    dma("sync", V("B0", 0, W), lambda: B("bw")[:], "ld5", (), ["B0"], 5500)
    dma("sync", V("V0", PAD, PAD + W), lambda: B("vv")[:], "ld6", (), ["V0"], 7000)

    def send(name, pairs, r, w, lat):
        fn = lambda q: remote(q, CTX["T"], CTX["topo"], CTX["core"], [(CTX["fwd"], d(), s()) for d, s in pairs], name)
        s = op("pool", fn, 400, r, (), sem="none", msg=(name, [d for d, s in pairs]))
        op("ext", None, 0, (), w, lat=(lat, "msg"), sem=name, inc="small", after=[s])

    def table(name, src, dst, off, lat):
        def fn(q):
            n = W // len(CTX["bulk"])
            return remote(q, CTX["T"], CTX["topo"], CTX["core"],
                          [(c, B(dst)[:, off + j * n:off + (j + 1) * n], B(src)[:, off + j * n:off + (j + 1) * n]) for j, c in enumerate(CTX["bulk"])], name)
        s = op("pool", fn, 600, [src], (), sem="none")
        op("ext", None, 0, (), [dst], lat=(lat, "tab"), sem=name, inc="bulk", after=[s])

    def iota(name, pat, cm, n, base=0):
        fl = SCRATCH[name][2] != I32
        def fn(q):
            a = B(name)[:, 0:n]
            return q.iota(a, pat, base, cm, allow_small_or_imprecise_dtypes=True) if fl else q.iota(a, pat, base, cm)
        op("pool", fn, 160 + 2.1 * n, (), [name])

    def sel(name, src, sa, sb, base, cm, cmp, fill, n=128):
        op("pool", lambda q: q.affine_select(B(name)[:, 0:n], B(src)[:, 0:n], [[sa, n // 16], [sb, 16]], cmp, fill, base, cm), 210 + 2.1 * n, [src], [name])
    iota("pi32", [[0, 1]], 1, 1)
    iota("NL", [[0, 8], [1, 16]], 0, 128)
    iota("ni", [[1, 128]], 0, 128)
    iota("NG", [[1, 8], [0, 16]], 0, 128)
    iota("NF", [[1, 144]], 0, 144)
    iota("ONEb", [[0, 128]], 0, 128, 1)
    iota("ONEf", [[0, 256]], 0, 256, 1)
    iota("NEG", [[0, 128]], 0, 128, -16384)
    iota("ZB", [[0, 128]], 0, 128)
    iota("ZF", [[0, 128]], 0, 128)
    iota("PRIO", [[0, 8], [256, 16]], 0, 128)
    NE, GE = ALU.not_equal, ALU.is_ge
    sel("RST", "ONEf", 0, 1, 0, 0, NE, 0.0, 256)
    for name, src, val in (("If", "ZF", 1.0), ("Ib", "ZB", 1.0), ("I2", "ZB", 2048.0), ("I8", "ZB", 8192.0)):
        sel(name, src, -16, -1, 0, 1, NE, val)
    sel("NJ", "ZB", -16, 1, -15, 1, NE, -1.0)
    sel("SEL", "ZF", -16, 0, -15, 1, NE, 1.0)
    for name, val in (("GT", 1.0), ("NGT", -1.0)):
        sel(name, "ZB", -1, 0, 0, 1, NE, val)
        sel(name, name, -1, 0, -8, 1, NE, val)
    sel("LAST", "GT", 0, 1, -15, 0, GE, 0.0)
    sel("NGTf", "ZF", -1, 0, 0, 1, NE, -1.0)
    sel("THS", "NGTf", 0, 1, 0, 0, NE, 0.0)
    send("mtok", [(V("tokn", 0, 16), V("toki", 32, 48))], ["toki"], ["tokn"], 9000)
    table("tK", "K0", "K1", PAD, 9000)
    table("tB", "B0", "B1", 0, 10000)
    table("tV", "V0", "V1", PAD, 12000)

    def ts(out, in0, s1, s2, o0, o1, n, r, w, tiles=(), c=1.0):
        def fn(q):
            a = s1() if not isinstance(s1, (int, float)) else s1
            b = s2() if not isinstance(s2, (int, float)) and s2 is not None else s2
            if o1 is None:
                return q.tensor_scalar(out(), in0(), a, None, o0)
            return q.tensor_scalar(out(), in0(), a, b, o0, o1)
        return dve(fn, n, r, w, tiles, c)

    def tt(out, in0, in1, o, n, r, w, tiles=(), c=1.0):
        return dve(lambda q: q.tensor_tensor(out(), in0(), in1(), o), n, r, w, tiles, c)

    def cp(out, in_, n, r, w, tiles=()):
        return dve(lambda q: q.tensor_copy(out(), in_()), n, r, w, tiles)

    def gcp(out, in_, n, r, w, tiles=(), c=1.0):
        return dve(lambda q: q.tensor_copy(out(), in_()), n, r, w, tiles, c)

    def acp(out, in_, n, r, w, tiles=(), c=1.0):
        return act(lambda q: q.activation(out(), in_(), ACT.Copy), n, r, w, tiles, c)

    def ms(ap, v, n, w, r=()):
        return dve(lambda q: q.memset(ap(), v), n, r, w)

    ts(V("pi32", 1, 2), V("pi32", 0, 1), 4, None, ALU.arith_shift_right, None, 1, ["pi32"], ["pi1"])
    ts(V("pi32", 2, 3), V("pi32", 0, 1), 15, None, ALU.bitwise_and, None, 1, ["pi32"], ["pi2"])
    cp(V("col", 1, 3), V("pi32", 1, 3), 2, ["pi1", "pi2"], ["col"])
    ts(V("col", 5, 6), C(1), 16.0, 15.0, ALU.mult, ALU.add, 1, ["col"], ["c5"])
    tt(V("col", 7, 8), C(5), C(2), ALU.subtract, 1, ["col", "c5"], ["c7"])
    cp(V("LIST", 0, 128), V("ni", 0, 128), 128, ["ni"], ["LIST"])
    EQ, MU = ALU.is_equal, ALU.mult
    ts(V("MASK", 0, 128), V("NL", 0, 128), C(2), None, EQ, None, 128, ["NL", "col"], ["MASK"])
    for name, val in (("BD", 1.0), ("NBD", -1.0), ("BDf", 1.0), ("NBDf", -1.0)):
        ts(V(name, 0, 128), V("NG", 0, 128), C(1), val, EQ, MU, 128, ["NG", "col"], [name])
    for name, val in (("G1", 1.0), ("G4", 4096.0), ("Gf", 1.0), ("NGf", -1.0)):
        ts(V(name, 0, 8), V("NL", 0, 8), C(1), val, EQ, MU, 8, ["NL", "col"], [name])
    ts(V("J", 0, 128), V("NF", 0, 128), C(7), None, EQ, None, 128, ["NF", "c7"], ["J"])
    ts(V("F", 0, 144), V("NF", 0, 144), C(5), None, EQ, None, 144, ["NF", "c5"], ["F"])
    sel("DM", "J", -16, 1, -14, 1, NE, -1.0)
    sel("DM", "DM", -16, 0, 0, 1, GE, 0.0)
    sel("LASTf", "BDf", 0, 1, -15, 0, GE, 0.0)
    ms(V("RS9", 0, 1), -1.0e6, 1, ["r9a"])
    ms(V("RS9", 1, 8), 0.0, 7, ["r9b"])
    ms(V("RS9", 8, 9), -80.0, 1, ["r9c"])
    ms(V("sc", 143, 864, 144), 0.0, 6, ["scz"])
    for name in ("K0", "K1", "V0", "V1"):
        ms(V(name, 0, PAD), 0.0, 8, [name + "z"])
    for j in range(POOLS["prod"]):
        ms(V("prod%d" % j, 0, PAD), 0.0, 8, [("pz", j)])
    PZ = [("pz", j) for j in range(POOLS["prod"])]
    cp(V8("thT", 0, 256), V8("thi", 0, 256), 256, ["thi"], ["thT"])
    cp(V("toku", 0, 32), V("toki", 0, 32), 32, ["toki"], ["toku"])
    cp(V("toku", 32, 48), V("tokn", 0, 16), 16, ["tokn"], ["tokv"])
    tl = tile("ps")
    def thr(tl=tl):
        res = []
        for h in range(2):
            res.append((P(tl)[:, 128 * h:128 * h + 128], B("thT")[0:8, 128 * h:128 * h + 128], B("THS")[0:8, :], True, False))
            res.append((P(tl)[:, 128 * h:128 * h + 128], B("ONEf")[0:1, 0:128], B("MASK")[0:1, 0:128], False, True))
        return res
    pe(thr, 2048, ["thT", "THS", "ONEf", "MASK"], [tl])
    act(lambda q, tl=tl: q.activation(B("thU")[:], P(tl)[:, 0:256], ACT.Identity, scale=-1.0), 256, (), ["thU"], [tl])

    def win(name, a, b, off, c, d):
        return lambda: B(name)[:, a:b].indirect(B(off)[:, c:d])

    cp(V("cL", 0, 16), V("curi", 0, 16), 16, ["curi"], [("cL", 0, 0), ("cL", 0, 1)])
    for h in range(2):
        tt(V("X0", 128 * h, 128 * h + 128), win("curi", 8 * h, 8 * h + 8, "LIST", 0, 8), V("MASK", 0, 128), MU, 128, ["curi", "LIST", "MASK"], [("cT", 0, h)], c=GA)
        acp(V("q", 128 * h, 128 * h + 128), win("K0", PAD, PAD + W, "toku", 8 * h, 8 * h + 8), 128, ["K0", "toku"], [("q", 0, h)], c=GA)

    def crep(t, neg, o, n):
        if t == 0:
            return B("NBDf" if neg else "BDf")[:], B("X0")[:, o:o + n]
        return B("NGT" if neg else "GT")[0:16, :], B("cT")[0:16, o:o + n]

    def big(t, hs, name, tab, zero, offb, qr):
        pr = qr["pr"][name]
        for c in range(2 * hs[0], 2 * hs[-1] + 2):
            a = PAD if not zero else 0
            tt(lambda c=c: P(pr)[:, PAD + CH * c:PAD + CH * (c + 1)], win(tab, a, PAD + W, offb, 256 * t + 64 * c, 256 * t + 64 * c + 64),
               lambda c=c: P(qr["q"])[:, CH * c:CH * (c + 1)], MU, CH,
               [tab, tab + "z", (offb, t, c // 2), ("qr", t, c)], [(name, t, c)], [pr, qr["q"]], c=GA)

    def uscore(tl, pr, h, col, g, first):
        res = []
        for i in range(16):
            a = PAD + 2048 * h
            res.append((P(tl)[:, col + i:col + 128:16], P(pr)[:, a + i:a + 2048:16], B(g)[:], first, first or i == 15))
        return res

    def step(t, pn, hs, qr):
        u0, n = 128 * hs[0], 128 * len(hs)
        o = 256 * t + u0
        K = lambda name: [(name, t, h) for h in hs]
        last = t == RO - 1
        l0, l1 = 16 * t + 8 * hs[0], 16 * t + 8 * hs[-1] + 8
        fc = 4 if t == 0 else 1
        if t > 0:
            tl = tile("ps")
            cp(V("cL", l0, l1), V("LA", l0 - 16, l1 - 16), 16, K("LA"), K("cL"))
            pe(lambda tl=tl: [(P(tl)[0:16, 128 * j:128 * j + 128], B("LH")[:, 32 * (t - 1) + 16 * h:32 * (t - 1) + 16 * h + 16], B("Ib")[:], True, True)
                              for j, h in enumerate(hs)], n, K("LA") + ["Ib"], [tl])
            acp(V8("cT", o, o + n, 16), lambda tl=tl: P(tl)[0:16, 0:n], n, (), K("cT"), [tl])
        acp(V("f", o, o + n), win("FW", 0, W, "cL", l0, l1), n, ["FW"] + K("cL"), K("f"), c=GA)
        tl = tile("ps")
        pe(lambda tl=tl: [(P(tl)[:, 0:n],) + crep(t, False, o, n) + (True, False),
                          (P(tl)[:, 0:n], B("J")[:], B("f")[:, o:o + n], False, True)], (1 + fc) * n, K("f") + K("cT") + ["GT", "BDf", "J"], [tl])
        cp(V("oS", o, o + n), lambda tl=tl: P(tl)[:, 0:n], n, (), K("oS"), [tl])
        for h in hs:
            a = 256 * t + 128 * h
            if (t, h) in OPT["qpool"]:
                for i in range(16):
                    op("pool", lambda q, a=a, h=h, i=i: q.affine_select(P(qr["q"])[:, 2048 * h + i:2048 * h + 2048:16], B("q")[:, a:a + 128], [[0, 128]],
                                                                       ALU.is_ge, 0.0, 0, 0),
                       480, [("q", t, h)], [("qr", t, 2 * h), ("qr", t, 2 * h + 1)], [qr["q"]], after=[len(ops) - 1] if i else [])
                continue
            for c in (2 * h, 2 * h + 1):
                acp(lambda c=c: P(qr["q"])[:, CH * c:CH * (c + 1)], win("q", a, a + 128, "LIST", 64 * (c % 2), 64 * (c % 2) + 64), CH,
                    [("q", t, h), "LIST"], [("qr", t, c)], [qr["q"]], c=GA)
        if t in OPT["early"]:
            pr, tq, cs = qr["pr"]["pS"], tile("ps"), range(2 * hs[0], 2 * hs[-1] + 2)
            for c in cs:
                acp(lambda c=c: P(pr)[:, PAD + CH * c:PAD + CH * (c + 1)], win("K0", PAD, PAD + W, "oS", 256 * t + 64 * c, 256 * t + 64 * c + 64), CH,
                    ["K0", ("oS", t, c // 2)], [("kg", t, c)], [pr], c=GA)
            pe(lambda: [(P(tq)[:, 0:n], B("Ib")[:], B("q")[:, o:o + n], True, True)], n, K("q") + ["Ib", ("kg", t, cs[-1])], [tq])
            for i in range(16):
                ap = lambda i=i: P(pr)[:, PAD + 16 * u0 + i:PAD + 16 * (u0 + n):16]
                tt(ap, ap, lambda: P(tq)[:, 0:n], MU, n, [("kg", t, c) for c in cs], [("pS", t, c) for c in cs], [pr, tq])
        else:
            big(t, hs, "pS", "K0", False, "oS", qr)
        sc = tile("ps")
        for j, h in enumerate(hs):
            a = 256 * t + 128 * h
            pe(lambda j=j, a=a: [(P(sc)[:, 256 + 128 * j:384 + 128 * j], B("f")[:, a:a + 128], B("DM")[:], True, False),
                                 (P(sc)[:, 256 + 128 * j:384 + 128 * j],) +
                                 ((B("X0")[:, a:a + 128], B("LASTf")[:]) if t == 0 else (B("cT")[0:16, a:a + 128], B("LAST")[0:16, :])) + (False, True)],
               128 + 128 * fc, [("f", t, h), ("cT", t, h), "DM", "LAST", "LASTf", ("pS", t, 2 * hs[0])], [sc])
        for j, h in enumerate(hs):
            pe(lambda j=j, h=h: uscore(sc, qr["pr"]["pS"], h, 128 * j, "G1", True), 1024 + 300,
               [("pS", t, 2 * h), ("pS", t, 2 * h + 1), "G1"], [sc, qr["pr"]["pS"]])
        tt(V("nh", o, o + n), lambda: P(sc)[:, 0:n], V("thU", u0, u0 + n), ALU.is_le, n, ["thU"], K("nh"), [sc])
        for j, h in enumerate(hs):
            a, s = 256 * t + 128 * h, 144 * (2 * t + h)
            dve(lambda q, a=a, s=s, j=j: q.tensor_tensor_scan(B("sc")[:, s:s + 128], B("nh")[:, a:a + 128], P(sc)[:, 256 + 128 * j:384 + 128 * j],
                                                              0.0, MU, ALU.add), 128, [("nh", t, h)], [("sc", t, h)], [sc])
        for h in hs:
            a, s, b, m, e = 256 * t + 128 * h, 144 * (2 * t + h), 16 * (2 * t + h), 32 * t + 16 * h, 16 * t + 8 * h
            dve(lambda q, s=s, b=b: q.tensor_tensor_scan(B("Bs")[:, b:b + 9], B("RS9")[:, 0:9], B("sc")[:, s + 15:s + 144:16], 0.0, ALU.add, ALU.max),
                9, [("sc", t, h), "scz", "r9a", "r9b", "r9c"], [("Bs", t, h)])
            ts(V("tm", e, e + 8), V("sc", s + 15, s + 128, 16), V("Bs", b + 8, b + 9), V("Bs", b + 7, b + 8), ALU.is_lt, MU, 8, [("Bs", t, h)], [("tm", t, h)])
            tt(V("bU", e, e + 8), V("sc", s + 15, s + 128, 16), V("tm", e, e + 8), ALU.max, 8, [("tm", t, h)], [("bU", t, h)])
            tt(V("X2", a, a + 128), win("bU", e, e + 8, "LIST", 0, 8), V("MASK", 0, 128), MU, 128, [("bU", t, h), "LIST", "MASK"], [("X2", t, h)], c=GA)
            cp(V("HL", m, m + 8), V("bU", e, e + 8), 8, [("bU", t, h)], [("hi", t, h)])
            tt(V("HL", m + 8, m + 16), V("bU", e, e + 8), V("HL", m, m + 8), ALU.subtract, 8, [("hi", t, h)], [("HL", t, h)])
        tl = tile("ps")
        pe(lambda tl=tl: [(P(tl)[:, 8 * j:8 * j + 8], B("X2")[:, 256 * t + 128 * h:256 * t + 128 * h + 128], B("Gf")[:], True, True)
                          for j, h in enumerate(hs)], 256 * len(hs), K("X2") + ["Gf"], [tl])
        cp(V("bL", l0, l1), lambda tl=tl: P(tl)[:, 0:8 * len(hs)], 16, (), K("bL"), [tl])
        if not last:
            acp(V("MA", l0, l1), lambda tl=tl: P(tl)[:, 0:8 * len(hs)], 16, (), K("bF"), [tl])
            send("mA%d%d" % (t, pn), [(V("LA", l0, l1), V("MA", l0, l1)), (V("LH", 2 * l0, 2 * l1), V("HL", 2 * l0, 2 * l1))],
                 K("HL") + K("bF"), [("LA", t + 1, h) for h in hs], 5500)
        tl = tile("ps")
        pe(lambda tl=tl: [(P(tl)[0:16, 128 * j:128 * j + 128], B("HL")[:, 32 * t + 16 * h:32 * t + 16 * h + 16], B("Ib")[:], True, True)
                          for j, h in enumerate(hs)], n, K("HL") + ["Ib"], [tl])
        acp(V8("bT", o, o + n, 16), lambda tl=tl: P(tl)[0:16, 0:n], n, (), K("bT"), [tl])
        for k in range(2):
            read(t, hs, k, qr)
        if not last:
            cp(V("ki", l0, l1), V("k0", o + 15, o + n, 16), 16, K("k0"), K("ki"))
            ts(V("ds", l0, l1), V("ki", l0, l1), 255, None, ALU.bitwise_and, None, 16, K("ki"), K("ds"))
            for h in hs:
                a, e = 256 * t + 128 * h, 16 * t + 8 * h
                tt(V("X3", a, a + 128), win("ds", e, e + 8, "LIST", 0, 8), V("MASK", 0, 128), MU, 128, [("ds", t, h), "LIST", "MASK"], [("X3", t, h)], c=GA)
            tl = tile("ps")
            def car(tl=tl):
                res = []
                for j, h in enumerate(hs):
                    a = 256 * t + 128 * h
                    res.append((P(tl)[:, 8 * j:8 * j + 8], B("X2")[:, a:a + 128], B("Gf")[:], True, False))
                    res.append((P(tl)[:, 8 * j:8 * j + 8], B("X3")[:, a:a + 128], B("NGf")[:], False, True))
                return res
            pe(car, 512 * len(hs), K("X2") + K("X3") + ["Gf", "NGf"], [tl])
            cp(V("fL", l0, l1), lambda tl=tl: P(tl)[:, 0:8 * len(hs)], 16, (), K("fL"), [tl])
            acp(V("kt", o, o + n), win("K1", PAD, PAD + W, "toku", 16 + l0, 16 + l1), n, ["K1", "toku" if t == 0 else "tokv"], K("kt"), c=GA)
            tt(V("qn", o, o + n), win("K0", PAD, PAD + W, "fL", l0, l1), V("kt", o, o + n), ALU.max, n, K("fL") + K("kt") + ["K0"], K("qn"), c=GA)
            send("mB%d%d" % (t, pn), [(V("q", 256 + o, 256 + o + n), V("qn", o, o + n))], K("qn"), [("q", t + 1, h) for h in hs], 6000)
        tt(V("mk", l0, l1), V("k0", o + 15, o + n, 16), V("k1", o + 15, o + n, 16), ALU.max, 16, K("k0") + K("k1"), K("mk"))
        ts(V("mi", l0, l1), V("mk", l0, l1), 1.0 / 4096, -0.47, MU, ALU.add, 16, K("mk"), K("mi"))
        cp(V("mf", l0, l1), V("mi", l0, l1), 16, K("mi"), K("mf"))
        tl = tile("ps")
        pe(lambda tl=tl: [(P(tl)[0:8, 128 * j:128 * j + 128], B("mf")[:, 16 * t + 8 * h:16 * t + 8 * h + 8], B("If")[:], True, True)
                          for j, h in enumerate(hs)], 512 * len(hs), K("mf") + ["If"], [tl], K("mP"))
        acp(V8("mT", o, o + n), lambda tl=tl: P(tl)[0:8, 0:n], n, (), K("mT"), [tl])
        dma("sync", lambda: B("ym")[:, o:o + n], V8("mT", o, o + n), "om%d%d" % (t, pn), K("mT"), (), 2000)
        for k in range(2):
            finish(t, pn, hs, k, qr)
        tl = tile("ps")
        pe(lambda tl=tl: [(P(tl)[0:8, 0:n], B("Gf")[:], B("w%d" % k)[:, o:o + n], k == 0, k == 1) for k in range(2)], 8 * n,
           K("w0") + K("w1") + ["Gf"], [tl])
        acp(V8("sT", o, o + n), lambda tl=tl: P(tl)[0:8, 0:n], n, (), K("sT"), [tl])
        dma("sync", lambda: B("ys")[:, o:o + n], V8("sT", o, o + n), "os%d%d" % (t, pn), K("sT"), (), 2000)

    def read(t, hs, k, qr):
        u0, n = 128 * hs[0], 128 * len(hs)
        o = 256 * t + u0
        K = lambda name: [(name, t, h) for h in hs]
        d, s, of, pn, kb = "d%d" % k, "s%d" % k, "o%d" % k, "p%d" % k, "k%d" % k
        pr = qr["pr"][pn]
        acp(V(d, o, o + n), win("B%d" % k, 0, W, "bL", 16 * t + 8 * hs[0], 16 * t + 8 * hs[-1] + 8), n, ["B%d" % k] + K("bL"), K(d), c=GA)
        ty, tp = tile("ps"), tile("ps")
        y = pe(lambda: [(P(ty)[:, 0:n],) + crep(t, True, o, n) + (True, False),
                        (P(ty)[:, 0:n], B("GT")[0:16, :], B("bT")[0:16, o:o + n], False, False),
                        (P(ty)[:, 0:n], B("NJ")[:], B(d)[:, o:o + n], False, True)], (6 if t == 0 else 3) * n,
               K("cT") + K("bT") + K(d) + ["GT", "NGT", "NBDf", "NJ"], [ty])
        act(lambda q: q.activation(B(s)[:, o:o + n], P(ty)[:, 0:n], ACT.Sign, bias=-0.5), n, (), K(s), [ty])
        pe(lambda: [(P(tp)[:, 0:n], B("GT")[0:16, :], B("bT")[0:16, o:o + n], True, False),
                    (P(tp)[:, 0:n], B("NJ")[:], B(d)[:, o:o + n], False, False),
                    (P(tp)[:, 0:n], B("I2")[:], B(s)[:, o:o + n], False, True)], 3 * n, K("bT") + K(d) + K(s) + ["I2"], [tp])
        ts(V(of, o, o + n), lambda: P(tp)[:, 0:n], float(PAD - 2048), 0.0, ALU.add, ALU.max, n, (), K(of), [tp])
        big(t, hs, pn, "K%d" % k, True, of, qr)
        tk = tile("ps")
        tag = k == 0 and t < RO - 1
        for j, h in enumerate(hs):
            a = 256 * t + 128 * h
            def keys(j=j, h=h, a=a):
                res = []
                if tag:
                    res = [(P(tk)[:, 128 * j:128 * j + 128], B(d)[:, a:a + 128], B("J")[:], True, False),
                           (P(tk)[:, 128 * j:128 * j + 128], B("ONEb")[0:1, :], B("PRIO")[0:1, :], False, False)]
                return res + uscore(tk, pr, h, 128 * j, "G4", not tag)
            pe(keys, 1024 + 300 + 256 * tag, [(pn, t, 2 * h), (pn, t, 2 * h + 1), "G4", (d, t, h), "J", "ONEb", "PRIO"], [tk, pr])
        dve(lambda q: q.tensor_tensor_scan(B(kb)[:, o:o + n], B("RST")[:, 0:n], P(tk)[:, 0:n], 0.0, MU, ALU.max), n, ["RST"], K(kb), [tk])
        st = qr["st"][k]
        for c in range(2 * hs[0], 2 * hs[-1] + 2):
            td, tr, tv = tile("pd"), tile("rt"), tile("vg")
            def diff(c=c, td=td):
                res = []
                for j in range(CH // 512):
                    a = PAD + CH * c + 512 * j
                    res.append((P(td)[:, 512 * j:512 * j + 512], B("BD")[:], P(pr)[:, a - 1:a + 511], True, False))
                    res.append((P(td)[:, 512 * j:512 * j + 512], B("NBD")[:], P(pr)[:, a:a + 512], False, False))
                    res.append((P(td)[:, 512 * j:512 * j + 512:16], B("NEG")[0:1, :], B("ONEb")[0:1, 0:32], False, True))
                return res
            pe(diff, 2 * CH + 200, [(pn, t, c), "BD", "NBD", "NEG", "ONEb"] + PZ + ([(pn, t, c - 1)] if c else []), [td, pr])
            act(lambda q, td=td, tr=tr: q.activation(P(tr)[:], P(td)[:], ACT.Exp, scale=1.0 / 128), CH, (), [("r", k, t, c)], [td, tr])
            (gcp if (t, k, c) in OPT["vdve"] else acp)(lambda tv=tv: P(tv)[:], win("V%d" % k, 0, PAD + W, of, 256 * t + 64 * c, 256 * t + 64 * c + 64), CH,
                ["V%d" % k, "V%dz" % k, (of, t, c // 2)], [("vg", k, t, c)], [tv], c=GA)
            dve(lambda q, c=c, tr=tr, tv=tv: q.tensor_tensor_scan(P(st)[:, CH * c:CH * (c + 1)], P(tr)[:], P(tv)[:], 0.0, MU, ALU.add), CH,
                [("r", k, t, c), ("vg", k, t, c)], [("st", k, t, c)], [tr, tv, st])

    def finish(t, part, hs, k, qr):
        u0, n = 128 * hs[0], 128 * len(hs)
        o = 256 * t + u0
        K = lambda name: [(name, t, h) for h in hs]
        cs = range(2 * hs[0], 2 * hs[-1] + 2)
        pr, st, pn, w = qr["pr"]["p%d" % k], qr["st"][k], "p%d" % k, "w%d" % k
        tl = tile("ps")
        def nsc(i0, i1):
            a = PAD + 16 * u0
            return [(P(tl)[:, 0:n], B("F")[:, 15 - i:143 - i], P(pr)[:, a + i:a + 16 * n:16], i == 0, False) for i in range(i0, i1)]
        for i in range(0, 16, 4):
            pe(lambda i=i: nsc(i, i + 4), 4 * n + 60, K("mP") + [(pn, t, c) for c in cs] + ["F"], [tl, pr])
        pe(lambda: [(P(tl)[:, 0:n], B("I8")[:], B("s%d" % k)[:, o:o + n], False, False),
                    (P(tl)[:, 0:n], B("NGTf")[0:8, :], B("mT")[0:8, o:o + n], False, True)], 5 * n, K("s%d" % k) + K("mT") + ["I8", "NGTf"], [tl])
        act(lambda q: q.activation(B(w)[:, o:o + n], P(tl)[:, 0:n], ACT.Exp, bias=-64.0, scale=1.0 / 128), n, (), K(w), [tl])
        te = tile("ps")
        pe(lambda: [(P(te)[:, 256:256 + n], B("SEL")[:], B(w)[:, o:o + n], True, True)], 4 * n, K(w) + ["SEL", ("st", k, t, cs[-1] - 1)], [te])
        out = V("x0", o, o + n) if k == 0 else (lambda: P(te)[:, 0:n])
        tt(out, lambda: P(st)[:, 16 * u0 + 15:16 * (u0 + n):16], lambda: P(te)[:, 256:256 + n], MU, n,
           [("st", k, t, c) for c in cs] + (K("x0") if k else []), K("x%d" % k), [te, st])
        if k == 1:
            tt(V("x0", o, o + n), V("x0", o, o + n), out, ALU.add, n, K("x0") + K("x1"), K("A"), [te])
            dma("sync", lambda: B("ya")[:, o:o + n], V("x0", o, o + n), "oa%d%d" % (t, part), K("A"), (), 2500)

    for t in range(RO):
        qr = {"q": tile("qrep"), "pr": {"pS": tile("prod"), "p0": tile("prod"), "p1": tile("prod")}, "st": [tile("st"), tile("st")]}
        for pn, hs in enumerate(OPT["parts"][t]):
            step(t, pn, hs, qr)
    return ops


def price(ops, M):
    for o in ops:
        cf, e = o["cf"], o["eng"]
        if not isinstance(cf, tuple):
            o["cost"] = cf
        elif e == "pe":
            o["cost"] = 60 + cf[0] * M["pe"]
        else:
            o["cost"] = M[e] + cf[0] * M["cyc"] * (M["g"] if cf[1] == "g" else cf[1])
        o["lat"] = o["lf"][0] * M[o["lf"][1]]


def gap(ops, o, d, M):
    both = ops[d]["eng"] == o["eng"]
    return 0.0 if (both and (o["eng"] == "pe" or d in o["soft"])) or o["eng"] == "ext" else M["same"] if both else M["cross"]


def schedule(ops, M):
    n = len(ops)
    price(ops, M)
    noise = np.random.RandomState(OPT["seed"]).uniform(-1.0, 1.0, n) * OPT["noise"]
    for s in OPT["moves"]:
        r = np.random.RandomState(s)
        k = r.randint(1, 12)
        noise[r.randint(0, n, k)] += r.uniform(-1.0, 1.0, k) * r.choice([500.0, 2000.0, 6000.0])
    succ = [[] for _ in range(n)]
    for o in ops:
        o["all"] = sorted(o["deps"] | o["time"])
        for d in o["all"]:
            succ[d].append(o["n"])
    prio = [0.0] * n
    for o in reversed(ops):
        prio[o["n"]] = o["cost"] + o["lat"] + max([prio[s] + 100 for s in succ[o["n"]]] + [0.0])
    prio = [p + float(x) + (1e6 if o["sem"] == "none" else 0.0) for p, x, o in zip(prio, noise, ops)]
    left = [len(o["all"]) for o in ops]
    ready = [o["n"] for o in ops if left[o["n"]] == 0]
    fin, free, order, base = {}, {}, [], {}
    tenant = {p: [None] * c for p, c in POOLS.items()}
    while ready:
        cand = []
        for j in ready:
            o = ops[j]
            if j not in base:
                base[j] = max([fin[d] + gap(ops, o, d, M) for d in o["all"]] + [0.0])
            st = max(base[j], free.get(o["eng"], 0.0) if o["eng"] != "ext" else 0.0)
            take, ok = [], True
            for tl in o["tiles"]:
                if tl["phys"] is None:
                    best = None
                    for s, old in enumerate(tenant[tl["pool"]]):
                        if old is None or all(u in fin for u in old["ops"]):
                            tm = 0.0 if old is None else max(fin[u] for u in old["ops"]) + M["cross"]
                            if best is None or tm < best[0]:
                                best = (tm, s)
                    if best is None:
                        ok = False
                        break
                    st = max(st, best[0])
                    take.append((tl, best[1]))
                else:
                    st = max(st, tl["since"])
            if ok:
                cand.append((st, j, take))
        if not cand:
            return None, 1e9
        first = min(cand, key=lambda c: (c[0], -prio[c[1]]))
        eng = ops[first[1]]["eng"]
        st, j, take = max([c for c in cand if ops[c[1]]["eng"] == eng and c[0] <= first[0] + OPT["slack"]], key=lambda c: prio[c[1]])
        o = ops[j]
        for tl, s in take:
            old = tenant[tl["pool"]][s]
            tl["phys"], tl["prev"] = s, ([] if old is None else list(old["ops"]))
            tl["since"] = max([fin[u] + M["cross"] for u in tl["prev"]] + [0.0])
            tenant[tl["pool"]][s] = tl
        o["start"] = st
        fin[j] = st + o["cost"] + o["lat"]
        free[o["eng"]] = st + o["cost"]
        order.append(j)
        ready.remove(j)
        for s in succ[j]:
            left[s] -= 1
            if left[s] == 0:
                ready.append(s)
    return order, max(fin.values())


def links(ops):
    pred = [set(o["all"]) | set(u for tl in o["tiles"] for u in tl["prev"]) for o in ops]
    succ = [set() for _ in ops]
    for j, p in enumerate(pred):
        for d in p:
            succ[d].add(j)
    return pred, succ


def shift(ops, order, pred, succ, code):
    j, far, back = code // 16, code % 8 + 1, code // 8 % 2
    i, d = order.index(j), (-1 if back else 1)
    stop, k, to = (pred if back else succ)[j], i + d, i
    while far and 0 <= k < len(order) and order[k] not in stop:
        if ops[order[k]]["eng"] == ops[j]["eng"]:
            far, to = far - 1, k
        k += d
    if to == i:
        return None
    res = order[:i] + order[i + 1:]
    res.insert(to, j)
    return res


def plan():
    ops = build()
    order = schedule(ops, MODEL)[0]
    pred, succ = links(ops)
    n, data = len(ops), []
    eng = [["pe", "dve", "act", "pool", "sync", "ext"].index(o["eng"]) for o in ops]
    for ch in SPREAD:
        M = dict(MODEL)
        M.update(ch)
        price(ops, M)
        data.append(([o["cost"] for o in ops], [o["cost"] + o["lat"] for o in ops],
                     [[(d, gap(ops, o, d, M) if d in o["all"] else M["cross"]) for d in sorted(pred[o["n"]])] for o in ops]))

    def run(order):
        tot = []
        for c, l, p in data:
            fin, free = [0.0] * n, [0.0] * 6
            for j in order:
                e = eng[j]
                st = free[e] if e < 5 else 0.0
                for d, g in p[j]:
                    x = fin[d] + g
                    if x > st:
                        st = x
                fin[j] = st + l[j]
                free[e] = st + c[j]
            tot.append(max(fin))
        return tot
    now = run(order)
    best = (now, order)
    r = np.random.RandomState(OPT["seed"])
    for it, code in enumerate(r.randint(0, 16 * n, OPT["tries"]).tolist()):
        c = shift(ops, order, pred, succ, code) if eng[code // 16] < 5 else None
        if c is not None:
            v = run(c)
            if sum(v) <= sum(now) + OPT["heat"] * (1.0 - it / OPT["tries"]) ** 2:
                now, order = v, c
                if sum(v) < sum(best[0]):
                    best = (v, c)
    CTX["times"] = best[0]
    return ops, best[1]


def routes(T, topo, rank):
    rank %= len(T.cores)
    me, nxt, prv = T.cores[rank], T.cores[(rank + 1) % len(T.cores)], T.cores[rank - 1]
    ok = [c for c in topo.cores_of(me) if c != me and topo.may_write(c, nxt) and topo.may_write(c, prv)]
    ok.sort(key=lambda c: topo.die(c) != topo.die(me))
    return nxt, prv, ok[0], ok[1:4]


def rank_program(g, core, T, topo):
    if not PLAN:
        PLAN.extend(plan())
    ops, order = PLAN
    CTX.update(T=T, core=core, topo=topo)
    rank = T.rank_of(core)
    if rank is None:
        for r, me in enumerate(T.cores):
            nxt, prv, fwd, bulk = routes(T, topo, r)
            sent = 0
            if core == fwd:
                for j in order:
                    msg = ops[j]["msg"]
                    if msg is not None:
                        g.wait_ge(T.sem[msg[0]], len(topo.engines(me, core)))
                        sent += remote(g, T, topo, core, [(nxt, d(), d()) for d in msg[1]], msg[0])
            elif core in bulk:
                n = W // len(bulk)
                a = n * bulk.index(core)
                for sem, buf, off in (("tK", "K1", PAD), ("tB", "B1", 0), ("tV", "V1", PAD)):
                    g.wait_ge(T.sem[sem], bits(split(topo.engines(me, core), len(bulk))[0]))
                    ap = T[buf][:, off + a:off + a + n]
                    sent += remote(g, T, topo, core, [(prv, ap, ap)], sem)
            if sent:
                g.wait_ge(T.sem.sent, sent)
        return
    nxt, prv, fwd, bulk = routes(T, topo, rank)
    CTX.update(fwd=fwd, bulk=bulk)
    ext = {"small": len(topo.engines(routes(T, topo, rank - 1)[2], core)),
           "bulk": sum(len(topo.engines(c, core)) for c in routes(T, topo, rank + 1)[3])}
    queue = {"pe": g.tensor, "dve": g.vector, "act": g.scalar, "pool": g, "sync": g.sync}
    known = {e: {} for e in queue}
    total, mark, clock = {}, {}, {}
    place = {j: i for i, j in enumerate(order)}
    sent = 0
    for j in order:
        o = ops[j]
        eng = o["eng"]
        if eng == "ext":
            total[o["sem"]] = ext[o["inc"]]
            mark[j] = (o["sem"], ext[o["inc"]])
            clock[j] = {o["sem"]: ext[o["inc"]]}
            continue
        deps = set(o["deps"])
        for tl in o["tiles"]:
            deps |= set(tl["prev"])
        kn = known[eng]
        for d in sorted(deps, key=lambda d: -place[d]):
            if (eng == "pe" and ops[d]["eng"] == "pe") or d in o["soft"]:
                continue
            s, v = mark[d]
            if kn.get(s, 0) < v:
                queue[eng].wait_ge(T.sem[s], v)
                for a, b in clock[d].items():
                    kn[a] = max(kn.get(a, 0), b)
        ins = o["fn"](queue[eng])
        if o["sem"] == "none":
            sent += ins
            continue
        s = o["sem"] or eng
        total[s] = total.get(s, 0) + o["inc"]
        ins.then_inc(T.sem[s], o["inc"])
        mark[j] = (s, total[s])
        clock[j] = dict(kn)
        clock[j][s] = total[s]
    g.wait_ge(T.sem.sent, sent)
    for s, v in total.items():
        g.wait_ge(T.sem[s], v)
